import numpy as np
CORES = [21,29,37,45,53,61,69,77,85]
N = 9
TK = 128
D = 128 * N
EPS = 0.01
def setup_inputs(rng):
    return {"x": (rng.standard_normal((N, 128, TK), dtype=np.float32) * (0.5 + np.abs(rng.standard_normal((1, 1, TK), dtype=np.float32))) + rng.standard_normal((1, 1, TK), dtype=np.float32)), "w": (rng.standard_normal((N, 128, 128), dtype=np.float32) / 11)}
def setup_inputs_big(rng):
    d = setup_inputs(rng)
    for k in ("x", "w"): d[k] = (d[k].astype(np.float32) * 1048576.0).astype(d[k].dtype)
    return d
def setup_inputs_small(rng):
    d = setup_inputs(rng)
    for k in ("x", "w"): d[k] = (d[k].astype(np.float32) * (1 / 1048576.0)).astype(d[k].dtype)
    return d
def setup_inputs_apart(rng):
    d = setup_inputs(rng)
    f = (10.0 ** rng.permutation(np.linspace(-1.5, 1.5, N))).astype(np.float32).reshape(N, 1, 1)
    for k in ("x", "w"): d[k] = (d[k].astype(np.float32) * f).astype(d[k].dtype)
    return d
def setup_inputs_mixed(rng):
    d = setup_inputs(rng)
    f = (10.0 ** rng.uniform(-3, 3, (1, 1, TK))).astype(np.float32); shape = rng.integers(3, size=(1, 1, TK))
    for k in ("x",):
        x = d[k].astype(np.float32)
        m = x.mean(axis=(0, 1), keepdims=True); level = m + np.sign(x - m) * np.abs(x - m).mean(axis=(0, 1), keepdims=True) * rng.uniform(0.9, 1.1, x.shape).astype(np.float32)
        other = x * np.where(rng.random(x.shape) < 0.5, 0.1, 1.0).astype(np.float32)
        d[k] = (np.where(shape == 1, level, np.where(shape == 2, other, x)) * f).astype(d[k].dtype)
    return d
def reference(x, w):
    X = x.astype(np.float64)
    Z = X
    Z = Z / np.sqrt((Z ** 2).sum(axis=(0, 1)) / D + EPS)
    s = sum(w[r].astype(np.float64).T @ Z[r] for r in range(N)).astype(np.float32)
    return {"y": np.broadcast_to(s, (N,) + s.shape)}

@@ -1,0 +1,206 @@
+from concourse.bass import DstId, RemoteDMATransfer
+from concourse.mybir import AluOpType, ActivationFunctionType
+
+EPS = 0.01
+W = 129
+MAXSRC = 5
+
+ENG_R_OFF = 8
+ENG_R_ON = 4
+ENG_H_OFF = 8
+ENG_H_ON = 8
+
+SCRATCH = {
+    "xs": ("sbuf", [128, 128], "float32"),
+    "ws": ("sbuf", [128, 128], "float32"),
+    "xsq": ("sbuf", [128, 128], "float32"),
+    "onec": ("sbuf", [128, 1], "float32"),
+    "ones": ("sbuf", [128, 128], "float32"),
+    "ident": ("sbuf", [128, 128], "float32"),
+    "send": ("sbuf", [128, W], "float32"),
+    "hland": ("sbuf", [128, MAXSRC * W], "float32"),
+    "land": ("sbuf", [128, 2 * W], "float32"),
+    "tmp": ("sbuf", [128, 128], "float32"),
+    "rt": ("sbuf", [128, 1], "float32"),
+    "rs": ("sbuf", [128, 1], "float32"),
+    "diag": ("sbuf", [128, 128], "float32"),
+    "yo": ("sbuf", [128, 128], "float32"),
+    "psP": ("psum", [128, 512], "float32"),
+    "psA": ("psum", [128, 512], "float32"),
+    "psS": ("psum", [128, 512], "float32"),
+}
+SEMAPHORES = ["cst", "idn", "ldx", "ldw", "sqd", "mmP", "mmA", "blk", "sent", "harr", "hsent", "arr",
+              "f_rt", "f_tmp", "f_rs", "f_dg", "f_S", "f_y", "sty"]
+
+
+def _bits(mask):
+    return [b for b in range(mask.bit_length()) if (mask >> b) & 1]
+
+
+def _pick(mask, n, taken=0):
+    free = _bits(mask & ~taken)
+    m = 0
+    for b in free[:n]:
+        m |= 1 << b
+    return m
+
+
+def _count(mask):
+    return len(_bits(mask))
+
+
+def _plan(T, topo):
+    cores = list(T.cores)
+    chip_of = [topo.chip(c) for c in cores]
+    planes = []
+    for r, ch in enumerate(chip_of):
+        for p in planes:
+            c0 = chip_of[p[0]]
+            if c0 == ch or topo.same_plane(c0, ch):
+                p.append(r)
+                break
+        else:
+            planes.append([r])
+    pairs = []
+    for ch in chip_of:
+        mate = [m for m in range(topo.CHIPS) if topo.mates(ch, m)][0]
+        pr = sorted([ch, mate])
+        if pr not in pairs:
+            pairs.append(pr)
+    every = range(topo.CHIPS * topo.CORES_PER_CHIP)
+    helpers = []
+    for p, members in enumerate(planes):
+        c0 = chip_of[members[0]]
+        die = topo.die(cores[members[0]])
+        for pr in pairs:
+            hchip = [ch for ch in pr if ch == c0 or topo.same_plane(ch, c0)][0]
+            dests = [r for r in range(len(cores)) if chip_of[r] in pr]
+            cand = [c for c in every if topo.chip(c) == hchip and c not in cores and topo.die(c) == die
+                    and all(topo.may_write(c, cores[d]) for d in dests)]
+            helpers.append({"core": cand[0], "plane": p, "srcs": members, "dests": dests})
+    return cores, planes, helpers
+
+
+def _rank_transfers(topo, cores, helpers, p, r):
+    me = cores[r]
+    mine = [h["core"] for h in helpers if h["plane"] == p]
+    at = [i for i, c in enumerate(mine) if topo.chip(c) == topo.chip(me)][0]
+    off = [mine[(at + k) % len(mine)] for k in range(1, len(mine))]
+    m_off = 0
+    for c in off:
+        m_off = topo.mask(me, c) if m_off == 0 else (m_off & topo.mask(me, c))
+    m_off = _pick(m_off, ENG_R_OFF)
+    m_on = _pick(topo.mask(me, mine[at]), ENG_R_ON, m_off)
+    return [(off, m_off), ([mine[at]], m_on)]
+
+
+def _helper_transfers(topo, cores, h):
+    me = h["core"]
+    off = [d for d in h["dests"] if topo.chip(cores[d]) != topo.chip(me)]
+    on = [d for d in h["dests"] if topo.chip(cores[d]) == topo.chip(me)]
+    out = []
+    taken = 0
+    if off:
+        m = _pick(topo.mask(me, cores[off[0]]), ENG_H_OFF)
+        taken |= m
+        out.append((off, m))
+    if on:
+        other = [c for c in cores if topo.chip(c) != topo.chip(me)][0]
+        m = _pick(topo.mask(me, cores[on[0]]), ENG_H_ON, taken | topo.mask(me, other))
+        out.append((on, m))
+    return out
+
+
+def _dst(topo, c):
+    rid, pid, _ = topo.addr(c)
+    return DstId(rid=rid, pnc=pid)
+
+
+def rank_program(g, core, T, topo):
+    cores, planes, helpers = _plan(T, topo)
+    S = T.sem
+    n = len(cores)
+    rank = T.rank_of(core)
+
+    if rank is None:
+        hs = [h for h in helpers if h["core"] == core]
+        if not hs:
+            return
+        h = hs[0]
+        p = h["plane"]
+        need = 0
+        for r in h["srcs"]:
+            for dsts, m in _rank_transfers(topo, cores, helpers, p, r):
+                if core in dsts:
+                    need += _count(m)
+        g.wait_ge(S.harr, need)
+        srcs = [T.hland[:, i * W:(i + 1) * W] for i in range(len(h["srcs"]))]
+        trs = []
+        left = 0
+        for dsts, m in _helper_transfers(topo, cores, h):
+            trs.append(RemoteDMATransfer(dst_ids=[_dst(topo, cores[d]) for d in dsts], dma_engine_mask=m,
+                                         remote_sem=S.arr, srcs=srcs,
+                                         dsts=[T.land[:, p * W:(p + 1) * W] for d in dsts], alu_op=1))
+            left += _count(m)
+        g.remote_dma_fused(trs, local_sem=S.hsent)
+        g.wait_ge(S.hsent, left)
+        return
+
+    p = [i for i, mem in enumerate(planes) if rank in mem][0]
+    slot = planes[p].index(rank)
+    q = 1 - p
+    V, A, PE, SP = g.vector, g.scalar, g.tensor, g.sync
+
+    SP.dma_start(T.xs[:, :], T.x[:, :]).then_inc(S.ldx, 16)
+    A.dma_start(T.ws[:, :], T.w[:, :]).then_inc(S.ldw, 16)
+    V.memset(T.onec[:, :], 1.0 / (128 * n)).then_inc(S.cst, 1)
+    V.memset(T.ones[:, :], 1.0).then_inc(S.cst, 1)
+    g.wait_ge(S.cst, 2)
+    g.affine_select(T.ident[:, :], T.ones[:, :], [[-1, 128]], AluOpType.is_equal, 0.0, 0, 1).then_inc(S.idn, 1)
+
+    A.wait_ge(S.ldx, 16)
+    A.activation(T.xsq[:, :], T.xs[:, :], ActivationFunctionType.Square).then_inc(S.sqd, 1)
+    PE.wait_ge(S.ldx, 16)
+    PE.wait_ge(S.ldw, 16)
+    PE.matmul(T.psP[:, 0:128], T.ws[:, :], T.xs[:, :], start=True, stop=True).then_inc(S.mmP, 1)
+    PE.wait_ge(S.sqd, 1)
+    PE.wait_ge(S.cst, 2)
+    PE.matmul(T.psA[:, 0:1], T.xsq[:, :], T.onec[:, :], start=True, stop=True).then_inc(S.mmA, 1)
+    V.wait_ge(S.mmP, 1)
+    V.tensor_copy(T.send[:, 0:128], T.psP[:, 0:128]).then_inc(S.blk, 1)
+    V.wait_ge(S.mmA, 1)
+    V.tensor_scalar(T.send[:, 128:129], T.psA[:, 0:1], EPS / n, None, AluOpType.add).then_inc(S.blk, 1)
+
+    g.wait_ge(S.blk, 2)
+    trs = []
+    left = 0
+    for dsts, m in _rank_transfers(topo, cores, helpers, p, rank):
+        trs.append(RemoteDMATransfer(dst_ids=[_dst(topo, c) for c in dsts], dma_engine_mask=m, remote_sem=S.harr,
+                                     src=T.send[:, :], dsts=[T.hland[:, slot * W:(slot + 1) * W] for c in dsts]))
+        left += _count(m)
+    g.remote_dma_fused(trs, local_sem=S.sent)
+
+    need = 0
+    for h in helpers:
+        for dsts, m in _helper_transfers(topo, cores, h):
+            if rank in dsts:
+                need += _count(m)
+    A.wait_ge(S.arr, need)
+    A.activation(T.rt[:, :], T.land[:, p * W + 128:p * W + 129], ActivationFunctionType.Sqrt,
+                 bias=T.land[:, q * W + 128:q * W + 129], scale=1.0).then_inc(S.f_rt, 1)
+    V.wait_ge(S.arr, need)
+    V.tensor_tensor(T.tmp[:, :], T.land[:, 0:128], T.land[:, W:W + 128], AluOpType.add).then_inc(S.f_tmp, 1)
+    V.wait_ge(S.f_rt, 1)
+    V.reciprocal(T.rs[:, :], T.rt[:, :]).then_inc(S.f_rs, 1)
+    V.wait_ge(S.f_rs, 1)
+    V.wait_ge(S.idn, 1)
+    V.tensor_scalar(T.diag[:, :], T.ident[:, :], T.rs[:, 0:1], None, AluOpType.mult).then_inc(S.f_dg, 1)
+    PE.wait_ge(S.f_dg, 1)
+    PE.matmul(T.psS[:, 0:128], T.ones[:, :], T.diag[:, :], start=True, stop=True).then_inc(S.f_S, 1)
+    V.wait_ge(S.f_S, 1)
+    V.wait_ge(S.f_tmp, 1)
+    V.tensor_tensor(T.yo[:, :], T.tmp[:, :], T.psS[:, 0:128], AluOpType.mult).then_inc(S.f_y, 1)
+    SP.wait_ge(S.f_y, 1)
+    SP.dma_start(T.y[:, :], T.yo[:, :]).then_inc(S.sty, 16)
+    SP.wait_ge(S.sty, 16)
+    g.wait_ge(S.sent, left)

@@ -4,11 +4,7 @@ from concourse.mybir import AluOpType, ActivationFunctionType
 EPS = 0.01
 W = 129
 MAXSRC = 5
-
-ENG_R_OFF = 8
-ENG_R_ON = 4
-ENG_H_OFF = 8
-ENG_H_ON = 8
+ENG = 8
 
 SCRATCH = {
     "xs": ("sbuf", [128, 128], "float32"),
@@ -19,8 +15,10 @@ SCRATCH = {
     "ident": ("sbuf", [128, 128], "float32"),
     "send": ("sbuf", [128, W], "float32"),
     "hland": ("sbuf", [128, MAXSRC * W], "float32"),
-    "land": ("sbuf", [128, 2 * W], "float32"),
+    "land": ("sbuf", [128, 4 * W], "float32"),
     "tmp": ("sbuf", [128, 128], "float32"),
+    "a0": ("sbuf", [128, 1], "float32"),
+    "a1": ("sbuf", [128, 1], "float32"),
     "rt": ("sbuf", [128, 1], "float32"),
     "rs": ("sbuf", [128, 1], "float32"),
     "diag": ("sbuf", [128, 128], "float32"),
@@ -30,7 +28,7 @@ SCRATCH = {
     "psS": ("psum", [128, 512], "float32"),
 }
 SEMAPHORES = ["cst", "idn", "ldx", "ldw", "sqd", "mmP", "mmA", "blk", "sent", "harr", "hsent", "arr",
-              "f_rt", "f_tmp", "f_rs", "f_dg", "f_S", "f_y", "sty"]
+              "f_a0", "f_a1", "f_rt", "f_tmp", "f_rs", "f_dg", "f_S", "f_y", "sty"]
 
 
 def _bits(mask):
@@ -38,15 +36,10 @@ def _bits(mask):
 
 
 def _pick(mask, n, taken=0):
-    free = _bits(mask & ~taken)
     m = 0
-    for b in free[:n]:
+    for b in _bits(mask & ~taken)[:n]:
         m |= 1 << b
     return m
-
-
-def _count(mask):
-    return len(_bits(mask))
 
 
 def _plan(T, topo):
@@ -55,60 +48,53 @@ def _plan(T, topo):
     planes = []
     for r, ch in enumerate(chip_of):
         for p in planes:
-            c0 = chip_of[p[0]]
-            if c0 == ch or topo.same_plane(c0, ch):
+            if chip_of[p[0]] == ch or topo.same_plane(chip_of[p[0]], ch):
                 p.append(r)
                 break
         else:
             planes.append([r])
-    pairs = []
+    sites = []
     for ch in chip_of:
-        mate = [m for m in range(topo.CHIPS) if topo.mates(ch, m)][0]
-        pr = sorted([ch, mate])
-        if pr not in pairs:
-            pairs.append(pr)
+        pr = sorted([ch] + [m for m in range(topo.CHIPS) if topo.mates(ch, m)])
+        if pr not in sites:
+            sites.append(pr)
+    ns = len(sites)
+    at_site = [[r for r in range(len(cores)) if chip_of[r] in pr] for pr in sites]
     every = range(topo.CHIPS * topo.CORES_PER_CHIP)
-    helpers = []
+    send, role = {}, {}
     for p, members in enumerate(planes):
         c0 = chip_of[members[0]]
         die = topo.die(cores[members[0]])
-        for pr in pairs:
-            hchip = [ch for ch in pr if ch == c0 or topo.same_plane(ch, c0)][0]
-            dests = [r for r in range(len(cores)) if chip_of[r] in pr]
-            cand = [c for c in every if topo.chip(c) == hchip and c not in cores and topo.die(c) == die
-                    and all(topo.may_write(c, cores[d]) for d in dests)]
-            helpers.append({"core": cand[0], "plane": p, "srcs": members, "dests": dests})
-    return cores, planes, helpers
+        chips = [[ch for ch in pr if ch == c0 or topo.same_plane(ch, c0)][0] for pr in sites]
+
+        def free(ch, dests):
+            return [c for c in every if topo.chip(c) == ch and c not in cores and c not in role
+                    and topo.die(c) == die and all(topo.may_write(c, cores[d]) for d in dests)][0]
+
+        adder = []
+        for i in range(ns):
+            adder.append(free(chips[i], at_site[i]))
+            role[adder[i]] = ("add", p, [], at_site[i])
+        for r in members:
+            i = chips.index(chip_of[r])
+            off = [adder[(i + k) % ns] for k in range(1, ns - 1)]
+            for c in off + [adder[i]]:
+                role[c][2].append(r)
+            on = []
+            gap = sorted(at_site[(i - 1) % ns], key=lambda d: topo.may_write(cores[r], cores[d]))
+            for d in gap:
+                f = free(chip_of[r], [d])
+                role[f] = ("fwd", p, [r], [d])
+                on.append(f)
+            send[r] = (off, on + [adder[i]])
+    return cores, planes, send, role
 
 
-def _rank_transfers(topo, cores, helpers, p, r):
-    me = cores[r]
-    mine = [h["core"] for h in helpers if h["plane"] == p]
-    at = [i for i, c in enumerate(mine) if topo.chip(c) == topo.chip(me)][0]
-    off = [mine[(at + k) % len(mine)] for k in range(1, len(mine))]
-    m_off = 0
-    for c in off:
-        m_off = topo.mask(me, c) if m_off == 0 else (m_off & topo.mask(me, c))
-    m_off = _pick(m_off, ENG_R_OFF)
-    m_on = _pick(topo.mask(me, mine[at]), ENG_R_ON, m_off)
-    return [(off, m_off), ([mine[at]], m_on)]
-
-
-def _helper_transfers(topo, cores, h):
-    me = h["core"]
-    off = [d for d in h["dests"] if topo.chip(cores[d]) != topo.chip(me)]
-    on = [d for d in h["dests"] if topo.chip(cores[d]) == topo.chip(me)]
-    out = []
-    taken = 0
-    if off:
-        m = _pick(topo.mask(me, cores[off[0]]), ENG_H_OFF)
-        taken |= m
-        out.append((off, m))
-    if on:
-        other = [c for c in cores if topo.chip(c) != topo.chip(me)][0]
-        m = _pick(topo.mask(me, cores[on[0]]), ENG_H_ON, taken | topo.mask(me, other))
-        out.append((on, m))
-    return out
+def _masks(topo, me, off, on):
+    far = [c for c in range(topo.CHIPS * topo.CORES_PER_CHIP) if topo.chip(c) != topo.chip(me)][0]
+    m_off = _pick(topo.mask(me, off[0]), ENG) if off else 0
+    m_on = _pick(topo.mask(me, on[0]), ENG, topo.mask(me, far)) if on else 0
+    return m_off, m_on
 
 
 def _dst(topo, c):
@@ -117,38 +103,38 @@ def _dst(topo, c):
 
 
 def rank_program(g, core, T, topo):
-    cores, planes, helpers = _plan(T, topo)
+    cores, planes, send, role = _plan(T, topo)
     S = T.sem
     n = len(cores)
     rank = T.rank_of(core)
 
     if rank is None:
-        hs = [h for h in helpers if h["core"] == core]
-        if not hs:
+        if core not in role:
             return
-        h = hs[0]
-        p = h["plane"]
-        need = 0
-        for r in h["srcs"]:
-            for dsts, m in _rank_transfers(topo, cores, helpers, p, r):
-                if core in dsts:
-                    need += _count(m)
-        g.wait_ge(S.harr, need)
-        srcs = [T.hland[:, i * W:(i + 1) * W] for i in range(len(h["srcs"]))]
+        kind, p, srcs, dests = role[core]
+        g.wait_ge(S.harr, ENG * len(srcs))
+        aps = [T.hland[:, planes[p].index(r) * W:(planes[p].index(r) + 1) * W] for r in srcs]
+        slot = p if kind == "add" else 2 + p
+        off = [cores[d] for d in dests if topo.chip(cores[d]) != topo.chip(core)]
+        on = [cores[d] for d in dests if topo.chip(cores[d]) == topo.chip(core)]
+        m_off, m_on = _masks(topo, core, off, on)
         trs = []
-        left = 0
-        for dsts, m in _helper_transfers(topo, cores, h):
-            trs.append(RemoteDMATransfer(dst_ids=[_dst(topo, cores[d]) for d in dsts], dma_engine_mask=m,
-                                         remote_sem=S.arr, srcs=srcs,
-                                         dsts=[T.land[:, p * W:(p + 1) * W] for d in dsts], alu_op=1))
-            left += _count(m)
+        for dsts, m in ((off, m_off), (on, m_on)):
+            if dsts:
+                out = [T.land[:, slot * W:(slot + 1) * W] for c in dsts]
+                ids = [_dst(topo, c) for c in dsts]
+                if len(aps) > 1:
+                    trs.append(RemoteDMATransfer(dst_ids=ids, dma_engine_mask=m, remote_sem=S.arr, srcs=aps,
+                                                 dsts=out, alu_op=1))
+                else:
+                    trs.append(RemoteDMATransfer(dst_ids=ids, dma_engine_mask=m, remote_sem=S.arr, src=aps[0],
+                                                 dsts=out))
         g.remote_dma_fused(trs, local_sem=S.hsent)
-        g.wait_ge(S.hsent, left)
+        g.wait_ge(S.hsent, ENG * len(trs))
         return
 
     p = [i for i, mem in enumerate(planes) if rank in mem][0]
-    slot = planes[p].index(rank)
-    q = 1 - p
+    mine = planes[p].index(rank)
     V, A, PE, SP = g.vector, g.scalar, g.tensor, g.sync
 
     SP.dma_start(T.xs[:, :], T.x[:, :]).then_inc(S.ldx, 16)
@@ -172,24 +158,35 @@ def rank_program(g, core, T, topo):
     V.tensor_scalar(T.send[:, 128:129], T.psA[:, 0:1], EPS / n, None, AluOpType.add).then_inc(S.blk, 1)
 
     g.wait_ge(S.blk, 2)
-    trs = []
-    left = 0
-    for dsts, m in _rank_transfers(topo, cores, helpers, p, rank):
-        trs.append(RemoteDMATransfer(dst_ids=[_dst(topo, c) for c in dsts], dma_engine_mask=m, remote_sem=S.harr,
-                                     src=T.send[:, :], dsts=[T.hland[:, slot * W:(slot + 1) * W] for c in dsts]))
-        left += _count(m)
+    off, on = send[rank]
+    m_off, m_on = _masks(topo, core, off, on)
+    trs = [RemoteDMATransfer(dst_ids=[_dst(topo, c) for c in dsts], dma_engine_mask=m, remote_sem=S.harr,
+                             src=T.send[:, :], dsts=[T.hland[:, mine * W:(mine + 1) * W] for c in dsts])
+           for dsts, m in ((off, m_off), (on, m_on))]
     g.remote_dma_fused(trs, local_sem=S.sent)
 
-    need = 0
-    for h in helpers:
-        for dsts, m in _helper_transfers(topo, cores, h):
-            if rank in dsts:
-                need += _count(m)
+    slots = sorted((pl if kind == "add" else 2 + pl) for kind, pl, _, dests in role.values() if rank in dests)
+    need = ENG * len(slots)
+    P = [T.land[:, s * W:s * W + 128] for s in slots]
+    a = [T.land[:, s * W + 128:s * W + 129] for s in slots]
     A.wait_ge(S.arr, need)
-    A.activation(T.rt[:, :], T.land[:, p * W + 128:p * W + 129], ActivationFunctionType.Sqrt,
-                 bias=T.land[:, q * W + 128:q * W + 129], scale=1.0).then_inc(S.f_rt, 1)
     V.wait_ge(S.arr, need)
-    V.tensor_tensor(T.tmp[:, :], T.land[:, 0:128], T.land[:, W:W + 128], AluOpType.add).then_inc(S.f_tmp, 1)
+    if len(a) > 2:
+        V.tensor_tensor(T.a0[:, :], a[0], a[1], AluOpType.add).then_inc(S.f_a0, 1)
+        A.wait_ge(S.f_a0, 1) if len(a) == 3 else None
+        lo, hi = T.a0[:, :], a[2]
+    else:
+        lo, hi = a[0], a[1]
+    if len(a) > 3:
+        A.activation(T.a1[:, :], a[2], ActivationFunctionType.Identity, bias=a[3], scale=1.0).then_inc(S.f_a1, 1)
+        A.wait_ge(S.f_a1, 1)
+        A.wait_ge(S.f_a0, 1)
+        hi = T.a1[:, :]
+    A.activation(T.rt[:, :], lo, ActivationFunctionType.Sqrt, bias=hi, scale=1.0).then_inc(S.f_rt, 1)
+    V.tensor_tensor(T.tmp[:, :], P[0], P[1], AluOpType.add).then_inc(S.f_tmp, 1)
+    for k in range(2, len(P)):
+        V.wait_ge(S.f_tmp, k - 1)
+        V.tensor_tensor(T.tmp[:, :], T.tmp[:, :], P[k], AluOpType.add).then_inc(S.f_tmp, 1)
     V.wait_ge(S.f_rt, 1)
     V.reciprocal(T.rs[:, :], T.rt[:, :]).then_inc(S.f_rs, 1)
     V.wait_ge(S.f_rs, 1)
@@ -198,9 +195,9 @@ def rank_program(g, core, T, topo):
     PE.wait_ge(S.f_dg, 1)
     PE.matmul(T.psS[:, 0:128], T.ones[:, :], T.diag[:, :], start=True, stop=True).then_inc(S.f_S, 1)
     V.wait_ge(S.f_S, 1)
-    V.wait_ge(S.f_tmp, 1)
+    V.wait_ge(S.f_tmp, len(P) - 1)
     V.tensor_tensor(T.yo[:, :], T.tmp[:, :], T.psS[:, 0:128], AluOpType.mult).then_inc(S.f_y, 1)
     SP.wait_ge(S.f_y, 1)
     SP.dma_start(T.y[:, :], T.yo[:, :]).then_inc(S.sty, 16)
     SP.wait_ge(S.sty, 16)
-    g.wait_ge(S.sent, left)
+    g.wait_ge(S.sent, ENG * len(trs))

@@ -5,6 +5,7 @@ EPS = 0.01
 W = 129
 MAXSRC = 5
 ENG = 8
+NADD = 2
 
 SCRATCH = {
     "xs": ("sbuf", [128, 128], "float32"),
@@ -15,7 +16,8 @@ SCRATCH = {
     "ident": ("sbuf", [128, 128], "float32"),
     "send": ("sbuf", [128, W], "float32"),
     "hland": ("sbuf", [128, MAXSRC * W], "float32"),
-    "land": ("sbuf", [128, 4 * W], "float32"),
+    "land": ("sbuf", [128, 6 * W], "float32"),
+    "pre": ("sbuf", [128, W], "float32"),
     "tmp": ("sbuf", [128, 128], "float32"),
     "a0": ("sbuf", [128, 1], "float32"),
     "a1": ("sbuf", [128, 1], "float32"),
@@ -27,8 +29,8 @@ SCRATCH = {
     "psA": ("psum", [128, 512], "float32"),
     "psS": ("psum", [128, 512], "float32"),
 }
-SEMAPHORES = ["cst", "idn", "ldx", "ldw", "sqd", "mmP", "mmA", "blk", "sent", "harr", "hsent", "arr",
-              "f_a0", "f_a1", "f_rt", "f_tmp", "f_rs", "f_dg", "f_S", "f_y", "sty"]
+SEMAPHORES = ["cst", "idn", "ldx", "ldw", "sqd", "mmP", "mmA", "blk", "sent", "harr", "hsent", "arr", "arrd",
+              "f_pre", "f_a0", "f_a1", "f_rt", "f_tmp", "f_rs", "f_dg", "f_S", "f_y", "sty"]
 
 
 def _bits(mask):
@@ -74,27 +76,26 @@ def _plan(T, topo):
         adder = []
         for i in range(ns):
             adder.append(free(chips[i], at_site[i]))
-            role[adder[i]] = ("add", p, [], at_site[i])
+            role[adder[i]] = (p, [], [(d, p) for d in at_site[i]])
         for r in members:
             i = chips.index(chip_of[r])
-            off = [adder[(i + k) % ns] for k in range(1, ns - 1)]
+            off = [adder[(i + k) % ns] for k in range(1, NADD + 1)]
             for c in off + [adder[i]]:
-                role[c][2].append(r)
-            on = []
-            gap = sorted(at_site[(i - 1) % ns], key=lambda d: topo.may_write(cores[r], cores[d]))
-            for d in gap:
-                f = free(chip_of[r], [d])
-                role[f] = ("fwd", p, [r], [d])
-                on.append(f)
-            send[r] = (off, on + [adder[i]])
+                role[c][1].append(r)
+            raw = [(d, 2 + 2 * p + (ns - 1 - k)) for k in range(NADD + 1, ns) for d in at_site[(i + k) % ns]]
+            straight = [(d, s) for d, s in raw if d in members]
+            across = [(d, s) for d, s in raw if d not in members]
+            f = free(chip_of[r], [d for d, s in across])
+            role[f] = (p, [r], across)
+            send[r] = (off, f, straight, adder[i])
     return cores, planes, send, role
 
 
-def _masks(topo, me, off, on):
-    far = [c for c in range(topo.CHIPS * topo.CORES_PER_CHIP) if topo.chip(c) != topo.chip(me)][0]
-    m_off = _pick(topo.mask(me, off[0]), ENG) if off else 0
-    m_on = _pick(topo.mask(me, on[0]), ENG, topo.mask(me, far)) if on else 0
-    return m_off, m_on
+def _masks(topo, me):
+    every = range(topo.CHIPS * topo.CORES_PER_CHIP)
+    far = [c for c in every if topo.chip(c) != topo.chip(me)][0]
+    near = [c for c in every if topo.chip(c) == topo.chip(me) and c != me][0]
+    return _pick(topo.mask(me, far), ENG), _pick(topo.mask(me, near), ENG, topo.mask(me, far))
 
 
 def _dst(topo, c):
@@ -107,22 +108,23 @@ def rank_program(g, core, T, topo):
     S = T.sem
     n = len(cores)
     rank = T.rank_of(core)
+    m_off, m_on = _masks(topo, core)
+
+    def blk(buf, s):
+        return buf[:, s * W:(s + 1) * W]
 
     if rank is None:
         if core not in role:
             return
-        kind, p, srcs, dests = role[core]
+        p, srcs, outs = role[core]
         g.wait_ge(S.harr, ENG * len(srcs))
-        aps = [T.hland[:, planes[p].index(r) * W:(planes[p].index(r) + 1) * W] for r in srcs]
-        slot = p if kind == "add" else 2 + p
-        off = [cores[d] for d in dests if topo.chip(cores[d]) != topo.chip(core)]
-        on = [cores[d] for d in dests if topo.chip(cores[d]) == topo.chip(core)]
-        m_off, m_on = _masks(topo, core, off, on)
+        aps = [blk(T.hland, planes[p].index(r)) for r in srcs]
         trs = []
-        for dsts, m in ((off, m_off), (on, m_on)):
-            if dsts:
-                out = [T.land[:, slot * W:(slot + 1) * W] for c in dsts]
-                ids = [_dst(topo, c) for c in dsts]
+        for m, here in ((m_off, False), (m_on, True)):
+            sel = [(d, s) for d, s in outs if (topo.chip(cores[d]) == topo.chip(core)) == here]
+            if sel:
+                ids = [_dst(topo, cores[d]) for d, s in sel]
+                out = [blk(T.land, s) for d, s in sel]
                 if len(aps) > 1:
                     trs.append(RemoteDMATransfer(dst_ids=ids, dma_engine_mask=m, remote_sem=S.arr, srcs=aps,
                                                  dsts=out, alu_op=1))
@@ -158,31 +160,41 @@ def rank_program(g, core, T, topo):
     V.tensor_scalar(T.send[:, 128:129], T.psA[:, 0:1], EPS / n, None, AluOpType.add).then_inc(S.blk, 1)
 
     g.wait_ge(S.blk, 2)
-    off, on = send[rank]
-    m_off, m_on = _masks(topo, core, off, on)
-    trs = [RemoteDMATransfer(dst_ids=[_dst(topo, c) for c in dsts], dma_engine_mask=m, remote_sem=S.harr,
-                             src=T.send[:, :], dsts=[T.hland[:, mine * W:(mine + 1) * W] for c in dsts])
-           for dsts, m in ((off, m_off), (on, m_on))]
-    g.remote_dma_fused(trs, local_sem=S.sent)
+    off, fwd, straight, own = send[rank]
 
-    slots = sorted((pl if kind == "add" else 2 + pl) for kind, pl, _, dests in role.values() if rank in dests)
-    need = ENG * len(slots)
-    P = [T.land[:, s * W:s * W + 128] for s in slots]
-    a = [T.land[:, s * W + 128:s * W + 129] for s in slots]
-    A.wait_ge(S.arr, need)
-    V.wait_ge(S.arr, need)
-    if len(a) > 2:
-        V.tensor_tensor(T.a0[:, :], a[0], a[1], AluOpType.add).then_inc(S.f_a0, 1)
-        A.wait_ge(S.f_a0, 1) if len(a) == 3 else None
-        lo, hi = T.a0[:, :], a[2]
+    def to_helpers(cs, m):
+        return RemoteDMATransfer(dst_ids=[_dst(topo, c) for c in cs], dma_engine_mask=m, remote_sem=S.harr,
+                                 src=T.send[:, :], dsts=[blk(T.hland, mine) for c in cs])
+
+    g.remote_dma_fused([to_helpers(off, m_off), to_helpers([fwd], m_on)], local_sem=S.sent)
+    g.remote_dma_fused([RemoteDMATransfer(dst_ids=[_dst(topo, cores[d]) for d, s in straight], dma_engine_mask=m_off,
+                                          remote_sem=S.arrd, src=T.send[:, :],
+                                          dsts=[blk(T.land, s) for d, s in straight]),
+                        to_helpers([own], m_on)], local_sem=S.sent)
+
+    early = sorted(s for r in send for d, s in send[r][2] if d == rank)
+    late = sorted(s for pl, _, outs in role.values() for d, s in outs if d == rank)
+    V.wait_ge(S.arrd, ENG * len(early))
+    if len(early) > 1:
+        V.tensor_tensor(T.pre[:, :], blk(T.land, early[0]), blk(T.land, early[1]), AluOpType.add).then_inc(S.f_pre, 1)
+        V.wait_ge(S.f_pre, 1)
+        first = T.pre
+        base = 0
     else:
-        lo, hi = a[0], a[1]
-    if len(a) > 3:
-        A.activation(T.a1[:, :], a[2], ActivationFunctionType.Identity, bias=a[3], scale=1.0).then_inc(S.f_a1, 1)
+        first = T.land
+        base = early[0] * W
+    P = [first[:, base:base + 128]] + [T.land[:, s * W:s * W + 128] for s in late]
+    a = [first[:, base + 128:base + 129]] + [T.land[:, s * W + 128:s * W + 129] for s in late]
+    A.wait_ge(S.arr, ENG * len(late))
+    V.wait_ge(S.arr, ENG * len(late))
+    V.tensor_scalar(T.a0[:, :], a[0], a[1], a[2], AluOpType.add, AluOpType.add).then_inc(S.f_a0, 1)
+    hi = a[3]
+    if len(a) > 4:
+        A.activation(T.a1[:, :], a[3], ActivationFunctionType.Identity, bias=a[4], scale=1.0).then_inc(S.f_a1, 1)
         A.wait_ge(S.f_a1, 1)
-        A.wait_ge(S.f_a0, 1)
         hi = T.a1[:, :]
-    A.activation(T.rt[:, :], lo, ActivationFunctionType.Sqrt, bias=hi, scale=1.0).then_inc(S.f_rt, 1)
+    A.wait_ge(S.f_a0, 1)
+    A.activation(T.rt[:, :], T.a0[:, :], ActivationFunctionType.Sqrt, bias=hi, scale=1.0).then_inc(S.f_rt, 1)
     V.tensor_tensor(T.tmp[:, :], P[0], P[1], AluOpType.add).then_inc(S.f_tmp, 1)
     for k in range(2, len(P)):
         V.wait_ge(S.f_tmp, k - 1)
@@ -200,4 +212,4 @@ def rank_program(g, core, T, topo):
     SP.wait_ge(S.f_y, 1)
     SP.dma_start(T.y[:, :], T.yo[:, :]).then_inc(S.sty, 16)
     SP.wait_ge(S.sty, 16)
-    g.wait_ge(S.sent, ENG * len(trs))
+    g.wait_ge(S.sent, ENG * 4)

@@ -1,11 +1,13 @@
 from concourse.bass import DstId, RemoteDMATransfer
-from concourse.mybir import AluOpType, ActivationFunctionType
+from concourse.mybir import AluOpType, ActivationFunctionType, AxisListType
 
 EPS = 0.01
 W = 129
+WP = 132
 MAXSRC = 5
 ENG = 8
 NADD = 2
+SIDE = 5
 
 SCRATCH = {
     "xs": ("sbuf", [128, 128], "float32"),
@@ -16,21 +18,20 @@ SCRATCH = {
     "ident": ("sbuf", [128, 128], "float32"),
     "send": ("sbuf", [128, W], "float32"),
     "hland": ("sbuf", [128, MAXSRC * W], "float32"),
-    "land": ("sbuf", [128, 6 * W], "float32"),
-    "pre": ("sbuf", [128, W], "float32"),
+    "land": ("sbuf", [128, (SIDE + 2) * WP], "float32"),
     "tmp": ("sbuf", [128, 128], "float32"),
-    "a0": ("sbuf", [128, 1], "float32"),
-    "a1": ("sbuf", [128, 1], "float32"),
-    "rt": ("sbuf", [128, 1], "float32"),
-    "rs": ("sbuf", [128, 1], "float32"),
+    "tmp2": ("sbuf", [128, 128], "float32"),
+    "at": ("sbuf", [128, 1], "float32"),
+    "ra": ("sbuf", [128, 1], "float32"),
+    "rep": ("sbuf", [128, 128], "float32"),
     "diag": ("sbuf", [128, 128], "float32"),
     "yo": ("sbuf", [128, 128], "float32"),
     "psP": ("psum", [128, 512], "float32"),
     "psA": ("psum", [128, 512], "float32"),
     "psS": ("psum", [128, 512], "float32"),
 }
-SEMAPHORES = ["cst", "idn", "ldx", "ldw", "sqd", "mmP", "mmA", "blk", "sent", "harr", "hsent", "arr", "arrd",
-              "f_pre", "f_a0", "f_a1", "f_rt", "f_tmp", "f_rs", "f_dg", "f_S", "f_y", "sty"]
+SEMAPHORES = ["cst", "idn", "ldx", "ldw", "sqd", "mmP", "mmA", "blk", "sent", "harr", "hsent", "arr",
+              "f_pre", "f_at", "f_ra", "f_rep", "f_tmp", "f_dg", "f_S", "f_y", "sty"]
 
 
 def _bits(mask):
@@ -76,19 +77,35 @@ def _plan(T, topo):
         adder = []
         for i in range(ns):
             adder.append(free(chips[i], at_site[i]))
-            role[adder[i]] = (p, [], [(d, p) for d in at_site[i]])
+            role[adder[i]] = (p, [], list(at_site[i]))
         for r in members:
             i = chips.index(chip_of[r])
             off = [adder[(i + k) % ns] for k in range(1, NADD + 1)]
             for c in off + [adder[i]]:
                 role[c][1].append(r)
-            raw = [(d, 2 + 2 * p + (ns - 1 - k)) for k in range(NADD + 1, ns) for d in at_site[(i + k) % ns]]
-            straight = [(d, s) for d, s in raw if d in members]
-            across = [(d, s) for d, s in raw if d not in members]
-            f = free(chip_of[r], [d for d, s in across])
+            raw = [d for k in range(NADD + 1, ns) for d in at_site[(i + k) % ns]]
+            across = [d for d in raw if d not in members]
+            f = free(chip_of[r], across)
             role[f] = (p, [r], across)
-            send[r] = (off, f, straight, adder[i])
-    return cores, planes, send, role
+            send[r] = (off, f, [d for d in raw if d in members], adder[i])
+    nl = [0] * len(cores)
+    for c in sorted(role):
+        p, srcs, outs = role[c]
+        new = []
+        for d in outs:
+            new.append((d, nl[d]))
+            nl[d] += 1
+        role[c] = (p, srcs, new)
+    many = [sum(d in send[r][2] for r in send) for d in range(len(cores))]
+    seen = [0] * len(cores)
+    for r in sorted(send):
+        off, f, straight, own = send[r]
+        new = []
+        for d in straight:
+            new.append((d, nl[d] if many[d] == 1 else SIDE + seen[d]))
+            seen[d] += 1
+        send[r] = (off, f, new, own)
+    return cores, planes, send, role, nl
 
 
 def _masks(topo, me):
@@ -104,27 +121,31 @@ def _dst(topo, c):
 
 
 def rank_program(g, core, T, topo):
-    cores, planes, send, role = _plan(T, topo)
+    cores, planes, send, role, nl = _plan(T, topo)
     S = T.sem
     n = len(cores)
     rank = T.rank_of(core)
     m_off, m_on = _masks(topo, core)
+    ADD, MUL = AluOpType.add, AluOpType.mult
 
-    def blk(buf, s):
-        return buf[:, s * W:(s + 1) * W]
+    def hblk(s):
+        return T.hland[:, s * W:(s + 1) * W]
+
+    def lblk(s):
+        return T.land[:, s * WP:s * WP + W]
 
     if rank is None:
         if core not in role:
             return
         p, srcs, outs = role[core]
         g.wait_ge(S.harr, ENG * len(srcs))
-        aps = [blk(T.hland, planes[p].index(r)) for r in srcs]
+        aps = [hblk(planes[p].index(r)) for r in srcs]
         trs = []
         for m, here in ((m_off, False), (m_on, True)):
             sel = [(d, s) for d, s in outs if (topo.chip(cores[d]) == topo.chip(core)) == here]
             if sel:
                 ids = [_dst(topo, cores[d]) for d, s in sel]
-                out = [blk(T.land, s) for d, s in sel]
+                out = [lblk(s) for d, s in sel]
                 if len(aps) > 1:
                     trs.append(RemoteDMATransfer(dst_ids=ids, dma_engine_mask=m, remote_sem=S.arr, srcs=aps,
                                                  dsts=out, alu_op=1))
@@ -143,6 +164,7 @@ def rank_program(g, core, T, topo):
     A.dma_start(T.ws[:, :], T.w[:, :]).then_inc(S.ldw, 16)
     V.memset(T.onec[:, :], 1.0 / (128 * n)).then_inc(S.cst, 1)
     V.memset(T.ones[:, :], 1.0).then_inc(S.cst, 1)
+    V.wait_ge(S.cst, 2)
     g.wait_ge(S.cst, 2)
     g.affine_select(T.ident[:, :], T.ones[:, :], [[-1, 128]], AluOpType.is_equal, 0.0, 0, 1).then_inc(S.idn, 1)
 
@@ -157,59 +179,48 @@ def rank_program(g, core, T, topo):
     V.wait_ge(S.mmP, 1)
     V.tensor_copy(T.send[:, 0:128], T.psP[:, 0:128]).then_inc(S.blk, 1)
     V.wait_ge(S.mmA, 1)
-    V.tensor_scalar(T.send[:, 128:129], T.psA[:, 0:1], EPS / n, None, AluOpType.add).then_inc(S.blk, 1)
+    V.tensor_scalar(T.send[:, 128:129], T.psA[:, 0:1], EPS / n, None, ADD).then_inc(S.blk, 1)
 
     g.wait_ge(S.blk, 2)
     off, fwd, straight, own = send[rank]
+    g.remote_dma_fused([
+        RemoteDMATransfer(dst_ids=[_dst(topo, c) for c in off] + [_dst(topo, cores[d]) for d, s in straight],
+                          dma_engine_mask=m_off, remote_sem=S.harr, src=T.send[:, :],
+                          dsts=[hblk(mine) for c in off] + [lblk(s) for d, s in straight]),
+        RemoteDMATransfer(dst_ids=[_dst(topo, fwd), _dst(topo, own)], dma_engine_mask=m_on, remote_sem=S.harr,
+                          src=T.send[:, :], dsts=[hblk(mine), hblk(mine)]),
+    ], local_sem=S.sent)
 
-    def to_helpers(cs, m):
-        return RemoteDMATransfer(dst_ids=[_dst(topo, c) for c in cs], dma_engine_mask=m, remote_sem=S.harr,
-                                 src=T.send[:, :], dsts=[blk(T.hland, mine) for c in cs])
-
-    g.remote_dma_fused([to_helpers(off, m_off), to_helpers([fwd], m_on)], local_sem=S.sent)
-    g.remote_dma_fused([RemoteDMATransfer(dst_ids=[_dst(topo, cores[d]) for d, s in straight], dma_engine_mask=m_off,
-                                          remote_sem=S.arrd, src=T.send[:, :],
-                                          dsts=[blk(T.land, s) for d, s in straight]),
-                        to_helpers([own], m_on)], local_sem=S.sent)
-
-    early = sorted(s for r in send for d, s in send[r][2] if d == rank)
-    late = sorted(s for pl, _, outs in role.values() for d, s in outs if d == rank)
-    V.wait_ge(S.arrd, ENG * len(early))
-    if len(early) > 1:
-        V.tensor_tensor(T.pre[:, :], blk(T.land, early[0]), blk(T.land, early[1]), AluOpType.add).then_inc(S.f_pre, 1)
+    k = nl[rank]
+    early = sum(d == rank for r in send for d, s in send[r][2])
+    A.wait_ge(S.idn, 1)
+    V.wait_ge(S.harr, ENG * early)
+    if early > 1:
+        V.tensor_tensor(lblk(k), lblk(SIDE), lblk(SIDE + 1), ADD).then_inc(S.f_pre, 1)
         V.wait_ge(S.f_pre, 1)
-        first = T.pre
-        base = 0
-    else:
-        first = T.land
-        base = early[0] * W
-    P = [first[:, base:base + 128]] + [T.land[:, s * W:s * W + 128] for s in late]
-    a = [first[:, base + 128:base + 129]] + [T.land[:, s * W + 128:s * W + 129] for s in late]
-    A.wait_ge(S.arr, ENG * len(late))
-    V.wait_ge(S.arr, ENG * len(late))
-    V.tensor_scalar(T.a0[:, :], a[0], a[1], a[2], AluOpType.add, AluOpType.add).then_inc(S.f_a0, 1)
-    hi = a[3]
-    if len(a) > 4:
-        A.activation(T.a1[:, :], a[3], ActivationFunctionType.Identity, bias=a[4], scale=1.0).then_inc(S.f_a1, 1)
-        A.wait_ge(S.f_a1, 1)
-        hi = T.a1[:, :]
-    A.wait_ge(S.f_a0, 1)
-    A.activation(T.rt[:, :], T.a0[:, :], ActivationFunctionType.Sqrt, bias=hi, scale=1.0).then_inc(S.f_rt, 1)
-    V.tensor_tensor(T.tmp[:, :], P[0], P[1], AluOpType.add).then_inc(S.f_tmp, 1)
-    for k in range(2, len(P)):
-        V.wait_ge(S.f_tmp, k - 1)
-        V.tensor_tensor(T.tmp[:, :], T.tmp[:, :], P[k], AluOpType.add).then_inc(S.f_tmp, 1)
-    V.wait_ge(S.f_rt, 1)
-    V.reciprocal(T.rs[:, :], T.rt[:, :]).then_inc(S.f_rs, 1)
-    V.wait_ge(S.f_rs, 1)
-    V.wait_ge(S.idn, 1)
-    V.tensor_scalar(T.diag[:, :], T.ident[:, :], T.rs[:, 0:1], None, AluOpType.mult).then_inc(S.f_dg, 1)
+    P = [T.land[:, s * WP:s * WP + 128] for s in range(k + 1)]
+    V.wait_ge(S.arr, ENG * k)
+    V.tensor_reduce(T.at[:, :], T.land[:, 128:k * WP + W:WP], AxisListType.X, ADD).then_inc(S.f_at, 1)
+    A.wait_ge(S.f_at, 1)
+    A.activation(T.diag[:, :], T.ident[:, :], ActivationFunctionType.Sqrt, scale=T.at[:, 0:1]).then_inc(S.f_dg, 1)
+    V.wait_ge(S.f_at, 1)
+    V.reciprocal(T.ra[:, :], T.at[:, :]).then_inc(S.f_ra, 1)
+    V.tensor_tensor(T.tmp[:, :], P[0], P[1], ADD).then_inc(S.f_tmp, 1)
+    V.wait_ge(S.f_ra, 1)
+    V.tensor_scalar(T.rep[:, :], T.ones[:, :], T.ra[:, 0:1], None, MUL).then_inc(S.f_rep, 1)
+    V.tensor_tensor(T.tmp2[:, :], P[2], P[3], ADD).then_inc(S.f_tmp, 1)
+    V.wait_ge(S.f_tmp, 2)
+    V.tensor_tensor(T.tmp[:, :], T.tmp[:, :], T.tmp2[:, :], ADD).then_inc(S.f_tmp, 1)
+    V.wait_ge(S.f_tmp, 3)
+    if k + 1 > 4:
+        V.tensor_tensor(T.tmp[:, :], T.tmp[:, :], P[4], ADD).then_inc(S.f_tmp, 1)
+        V.wait_ge(S.f_tmp, 4)
+    PE.wait_ge(S.f_rep, 1)
     PE.wait_ge(S.f_dg, 1)
-    PE.matmul(T.psS[:, 0:128], T.ones[:, :], T.diag[:, :], start=True, stop=True).then_inc(S.f_S, 1)
+    PE.matmul(T.psS[:, 0:128], T.rep[:, :], T.diag[:, :], start=True, stop=True).then_inc(S.f_S, 1)
     V.wait_ge(S.f_S, 1)
-    V.wait_ge(S.f_tmp, len(P) - 1)
-    V.tensor_tensor(T.yo[:, :], T.tmp[:, :], T.psS[:, 0:128], AluOpType.mult).then_inc(S.f_y, 1)
+    V.tensor_tensor(T.yo[:, :], T.tmp[:, :], T.psS[:, 0:128], MUL).then_inc(S.f_y, 1)
     SP.wait_ge(S.f_y, 1)
     SP.dma_start(T.y[:, :], T.yo[:, :]).then_inc(S.sty, 16)
     SP.wait_ge(S.sty, 16)
-    g.wait_ge(S.sent, ENG * 4)
+    g.wait_ge(S.sent, ENG * 2)

@@ -21,6 +21,9 @@ SCRATCH = {
     "land": ("sbuf", [128, (SIDE + 2) * WP], "float32"),
     "tmp": ("sbuf", [128, 128], "float32"),
     "tmp2": ("sbuf", [128, 128], "float32"),
+    "cc": ("sbuf", [128, 1], "float32"),
+    "rc": ("sbuf", [128, 1], "float32"),
+    "dc2": ("sbuf", [128, 128], "float32"),
     "at": ("sbuf", [128, 1], "float32"),
     "ra": ("sbuf", [128, 1], "float32"),
     "rep": ("sbuf", [128, 128], "float32"),
@@ -31,7 +34,7 @@ SCRATCH = {
     "psS": ("psum", [128, 512], "float32"),
 }
 SEMAPHORES = ["cst", "idn", "ldx", "ldw", "sqd", "mmP", "mmA", "blk", "sent", "harr", "hsent", "arr",
-              "f_pre", "f_at", "f_ra", "f_rep", "f_tmp", "f_dg", "f_S", "f_y", "sty"]
+              "f_c", "f_rc", "f_k", "f_pre", "f_at", "f_ra", "f_t1", "f_t2", "f_dg", "f_S", "f_y", "sty"]
 
 
 def _bits(mask):
@@ -127,6 +130,7 @@ def rank_program(g, core, T, topo):
     rank = T.rank_of(core)
     m_off, m_on = _masks(topo, core)
     ADD, MUL = AluOpType.add, AluOpType.mult
+    SQRT = ActivationFunctionType.Sqrt
 
     def hblk(s):
         return T.hland[:, s * W:(s + 1) * W]
@@ -191,33 +195,44 @@ def rank_program(g, core, T, topo):
                           src=T.send[:, :], dsts=[hblk(mine), hblk(mine)]),
     ], local_sem=S.sent)
 
+    A.wait_ge(S.blk, 2)
+    A.activation(T.cc[:, :], T.send[:, 128:129], SQRT).then_inc(S.f_c, 1)
+    V.wait_ge(S.f_c, 1)
+    V.wait_ge(S.idn, 1)
+    V.reciprocal(T.rc[:, :], T.cc[:, :]).then_inc(S.f_rc, 1)
+    V.tensor_scalar(T.dc2[:, :], T.ident[:, :], T.cc[:, 0:1], T.cc[:, 0:1], MUL, MUL).then_inc(S.f_k, 1)
+    V.wait_ge(S.f_rc, 1)
+    V.tensor_scalar(T.rep[:, :], T.ones[:, :], T.rc[:, 0:1], None, MUL).then_inc(S.f_k, 1)
+    A.wait_ge(S.f_k, 2)
+    PE.wait_ge(S.f_k, 2)
+
     k = nl[rank]
     early = sum(d == rank for r in send for d, s in send[r][2])
-    A.wait_ge(S.idn, 1)
     V.wait_ge(S.harr, ENG * early)
     if early > 1:
         V.tensor_tensor(lblk(k), lblk(SIDE), lblk(SIDE + 1), ADD).then_inc(S.f_pre, 1)
         V.wait_ge(S.f_pre, 1)
     P = [T.land[:, s * WP:s * WP + 128] for s in range(k + 1)]
+
     V.wait_ge(S.arr, ENG * k)
     V.tensor_reduce(T.at[:, :], T.land[:, 128:k * WP + W:WP], AxisListType.X, ADD).then_inc(S.f_at, 1)
-    A.wait_ge(S.f_at, 1)
-    A.activation(T.diag[:, :], T.ident[:, :], ActivationFunctionType.Sqrt, scale=T.at[:, 0:1]).then_inc(S.f_dg, 1)
+    V.tensor_tensor(T.tmp2[:, :], P[k], P[k - 1], ADD).then_inc(S.f_t2, 1)
     V.wait_ge(S.f_at, 1)
     V.reciprocal(T.ra[:, :], T.at[:, :]).then_inc(S.f_ra, 1)
-    V.tensor_tensor(T.tmp[:, :], P[0], P[1], ADD).then_inc(S.f_tmp, 1)
-    V.wait_ge(S.f_ra, 1)
-    V.tensor_scalar(T.rep[:, :], T.ones[:, :], T.ra[:, 0:1], None, MUL).then_inc(S.f_rep, 1)
-    V.tensor_tensor(T.tmp2[:, :], P[2], P[3], ADD).then_inc(S.f_tmp, 1)
-    V.wait_ge(S.f_tmp, 2)
-    V.tensor_tensor(T.tmp[:, :], T.tmp[:, :], T.tmp2[:, :], ADD).then_inc(S.f_tmp, 1)
-    V.wait_ge(S.f_tmp, 3)
-    if k + 1 > 4:
-        V.tensor_tensor(T.tmp[:, :], T.tmp[:, :], P[4], ADD).then_inc(S.f_tmp, 1)
-        V.wait_ge(S.f_tmp, 4)
-    PE.wait_ge(S.f_rep, 1)
+    A.wait_ge(S.f_ra, 1)
+    A.activation(T.diag[:, :], T.dc2[:, :], SQRT, scale=T.ra[:, 0:1]).then_inc(S.f_dg, 1)
     PE.wait_ge(S.f_dg, 1)
     PE.matmul(T.psS[:, 0:128], T.rep[:, :], T.diag[:, :], start=True, stop=True).then_inc(S.f_S, 1)
+    V.tensor_tensor(T.tmp[:, :], P[0], P[1], ADD).then_inc(S.f_t1, 1)
+    V.wait_ge(S.f_t2, 1)
+    t2 = 1
+    for s in range(2, k - 1):
+        V.tensor_tensor(T.tmp2[:, :], T.tmp2[:, :], P[s], ADD).then_inc(S.f_t2, 1)
+        t2 += 1
+        V.wait_ge(S.f_t2, t2)
+    V.wait_ge(S.f_t1, 1)
+    V.tensor_tensor(T.tmp[:, :], T.tmp[:, :], T.tmp2[:, :], ADD).then_inc(S.f_t1, 1)
+    V.wait_ge(S.f_t1, 2)
     V.wait_ge(S.f_S, 1)
     V.tensor_tensor(T.yo[:, :], T.tmp[:, :], T.psS[:, 0:128], MUL).then_inc(S.f_y, 1)
     SP.wait_ge(S.f_y, 1)

@@ -33,7 +33,7 @@ SCRATCH = {
     "psA": ("psum", [128, 512], "float32"),
     "psS": ("psum", [128, 512], "float32"),
 }
-SEMAPHORES = ["cst", "idn", "ldx", "ldw", "sqd", "mmP", "mmA", "blk", "sent", "harr", "hsent", "arr",
+SEMAPHORES = ["cst", "idn", "ldx", "ldw", "xarr", "sqd", "mmP", "mmA", "blk", "sent", "harr", "hsent", "arr",
               "f_c", "f_rc", "f_k", "f_pre", "f_at", "f_ra", "f_t1", "f_t2", "f_dg", "f_S", "f_y", "sty"]
 
 
@@ -73,9 +73,9 @@ def _plan(T, topo):
         die = topo.die(cores[members[0]])
         chips = [[ch for ch in pr if ch == c0 or topo.same_plane(ch, c0)][0] for pr in sites]
 
-        def free(ch, dests):
+        def free(ch, dests, same=True):
             return [c for c in every if topo.chip(c) == ch and c not in cores and c not in role
-                    and topo.die(c) == die and all(topo.may_write(c, cores[d]) for d in dests)][0]
+                    and (topo.die(c) == die) == same and all(topo.may_write(c, cores[d]) for d in dests)][0]
 
         adder = []
         for i in range(ns):
@@ -88,9 +88,13 @@ def _plan(T, topo):
                 role[c][1].append(r)
             raw = [d for k in range(NADD + 1, ns) for d in at_site[(i + k) % ns]]
             across = [d for d in raw if d not in members]
-            f = free(chip_of[r], across)
-            role[f] = (p, [r], across)
-            send[r] = (off, f, [d for d in raw if d in members], adder[i])
+            f = free(chip_of[r], across[:1])
+            role[f] = (p, [r], across[:1])
+            f2 = None
+            if across[1:]:
+                f2 = free(chip_of[r], across[1:], False)
+                role[f2] = (p, [r], across[1:])
+            send[r] = (off, f, [d for d in raw if d in members], adder[i], f2)
     nl = [0] * len(cores)
     for c in sorted(role):
         p, srcs, outs = role[c]
@@ -102,12 +106,12 @@ def _plan(T, topo):
     many = [sum(d in send[r][2] for r in send) for d in range(len(cores))]
     seen = [0] * len(cores)
     for r in sorted(send):
-        off, f, straight, own = send[r]
+        off, f, straight, own, f2 = send[r]
         new = []
         for d in straight:
             new.append((d, nl[d] if many[d] == 1 else SIDE + seen[d]))
             seen[d] += 1
-        send[r] = (off, f, new, own)
+        send[r] = (off, f, new, own, f2)
     return cores, planes, send, role, nl
 
 
@@ -123,12 +127,33 @@ def _dst(topo, c):
     return DstId(rid=rid, pnc=pid)
 
 
+def _block(g, T, n, have_x, have_xw, ncst):
+    S = T.sem
+    V, A, PE = g.vector, g.scalar, g.tensor
+    for sem, v in have_x:
+        A.wait_ge(sem, v)
+    A.activation(T.xsq[:, :], T.xs[:, :], ActivationFunctionType.Square).then_inc(S.sqd, 1)
+    for sem, v in have_xw:
+        PE.wait_ge(sem, v)
+    PE.matmul(T.psP[:, 0:128], T.ws[:, :], T.xs[:, :], start=True, stop=True).then_inc(S.mmP, 1)
+    PE.wait_ge(S.sqd, 1)
+    PE.wait_ge(S.cst, ncst)
+    PE.matmul(T.psA[:, 0:1], T.xsq[:, :], T.onec[:, :], start=True, stop=True).then_inc(S.mmA, 1)
+    V.wait_ge(S.mmP, 1)
+    V.tensor_copy(T.send[:, 0:128], T.psP[:, 0:128]).then_inc(S.blk, 1)
+    V.wait_ge(S.mmA, 1)
+    V.tensor_scalar(T.send[:, 128:129], T.psA[:, 0:1], EPS / n, None, AluOpType.add).then_inc(S.blk, 1)
+
+
 def rank_program(g, core, T, topo):
     cores, planes, send, role, nl = _plan(T, topo)
     S = T.sem
     n = len(cores)
     rank = T.rank_of(core)
     m_off, m_on = _masks(topo, core)
+    half = ENG // 2
+    m_x = _pick(m_on, half)
+    m_w = _pick(m_on, half, m_x)
     ADD, MUL = AluOpType.add, AluOpType.mult
     SQRT = ActivationFunctionType.Sqrt
 
@@ -142,8 +167,14 @@ def rank_program(g, core, T, topo):
         if core not in role:
             return
         p, srcs, outs = role[core]
-        g.wait_ge(S.harr, ENG * len(srcs))
-        aps = [hblk(planes[p].index(r)) for r in srcs]
+        if core in [send[r][1] for r in send]:
+            g.vector.memset(T.onec[:, :], 1.0 / (128 * n)).then_inc(S.cst, 1)
+            _block(g, T, n, [(S.xarr, 2 * half)], [(S.xarr, 2 * half)], 1)
+            g.wait_ge(S.blk, 2)
+            aps = [T.send[:, :]]
+        else:
+            g.wait_ge(S.harr, ENG * len(srcs))
+            aps = [hblk(planes[p].index(r)) for r in srcs]
         trs = []
         for m, here in ((m_off, False), (m_on, True)):
             sel = [(d, s) for d, s in outs if (topo.chip(cores[d]) == topo.chip(core)) == here]
@@ -163,6 +194,7 @@ def rank_program(g, core, T, topo):
     p = [i for i, mem in enumerate(planes) if rank in mem][0]
     mine = planes[p].index(rank)
     V, A, PE, SP = g.vector, g.scalar, g.tensor, g.sync
+    off, twin, straight, own, fwd = send[rank]
 
     SP.dma_start(T.xs[:, :], T.x[:, :]).then_inc(S.ldx, 16)
     A.dma_start(T.ws[:, :], T.w[:, :]).then_inc(S.ldw, 16)
@@ -172,27 +204,25 @@ def rank_program(g, core, T, topo):
     g.wait_ge(S.cst, 2)
     g.affine_select(T.ident[:, :], T.ones[:, :], [[-1, 128]], AluOpType.is_equal, 0.0, 0, 1).then_inc(S.idn, 1)
 
-    A.wait_ge(S.ldx, 16)
-    A.activation(T.xsq[:, :], T.xs[:, :], ActivationFunctionType.Square).then_inc(S.sqd, 1)
-    PE.wait_ge(S.ldx, 16)
-    PE.wait_ge(S.ldw, 16)
-    PE.matmul(T.psP[:, 0:128], T.ws[:, :], T.xs[:, :], start=True, stop=True).then_inc(S.mmP, 1)
-    PE.wait_ge(S.sqd, 1)
-    PE.wait_ge(S.cst, 2)
-    PE.matmul(T.psA[:, 0:1], T.xsq[:, :], T.onec[:, :], start=True, stop=True).then_inc(S.mmA, 1)
-    V.wait_ge(S.mmP, 1)
-    V.tensor_copy(T.send[:, 0:128], T.psP[:, 0:128]).then_inc(S.blk, 1)
-    V.wait_ge(S.mmA, 1)
-    V.tensor_scalar(T.send[:, 128:129], T.psA[:, 0:1], EPS / n, None, ADD).then_inc(S.blk, 1)
+    g.wait_ge(S.ldx, 16)
+    g.wait_ge(S.ldw, 16)
+    g.remote_dma_fused([
+        RemoteDMATransfer(dst_ids=[_dst(topo, twin)], dma_engine_mask=m_x, remote_sem=S.xarr, src=T.xs[:, :],
+                          dsts=[T.xs[:, :]]),
+        RemoteDMATransfer(dst_ids=[_dst(topo, twin)], dma_engine_mask=m_w, remote_sem=S.xarr, src=T.ws[:, :],
+                          dsts=[T.ws[:, :]]),
+    ], local_sem=S.sent)
+
+    _block(g, T, n, [(S.ldx, 16)], [(S.ldx, 16), (S.ldw, 16)], 2)
 
     g.wait_ge(S.blk, 2)
-    off, fwd, straight, own = send[rank]
+    near = ([fwd] if fwd is not None else []) + [own]
     g.remote_dma_fused([
         RemoteDMATransfer(dst_ids=[_dst(topo, c) for c in off] + [_dst(topo, cores[d]) for d, s in straight],
                           dma_engine_mask=m_off, remote_sem=S.harr, src=T.send[:, :],
                           dsts=[hblk(mine) for c in off] + [lblk(s) for d, s in straight]),
-        RemoteDMATransfer(dst_ids=[_dst(topo, fwd), _dst(topo, own)], dma_engine_mask=m_on, remote_sem=S.harr,
-                          src=T.send[:, :], dsts=[hblk(mine), hblk(mine)]),
+        RemoteDMATransfer(dst_ids=[_dst(topo, c) for c in near], dma_engine_mask=m_on, remote_sem=S.harr,
+                          src=T.send[:, :], dsts=[hblk(mine) for c in near]),
     ], local_sem=S.sent)
 
     A.wait_ge(S.blk, 2)
@@ -238,4 +268,4 @@ def rank_program(g, core, T, topo):
     SP.wait_ge(S.f_y, 1)
     SP.dma_start(T.y[:, :], T.yo[:, :]).then_inc(S.sty, 16)
     SP.wait_ge(S.sty, 16)
-    g.wait_ge(S.sent, ENG * 2)
+    g.wait_ge(S.sent, 2 * half + 2 * ENG)

from concourse.bass import DstId, RemoteDMATransfer
from concourse.mybir import AluOpType, ActivationFunctionType, AxisListType

EPS = 0.01
W = 129
WP = 132
MAXSRC = 5
ENG = 8
NADD = 2
SIDE = 5

SCRATCH = {
    "xs": ("sbuf", [128, 128], "float32"),
    "ws": ("sbuf", [128, 128], "float32"),
    "xsq": ("sbuf", [128, 128], "float32"),
    "onec": ("sbuf", [128, 1], "float32"),
    "ones": ("sbuf", [128, 128], "float32"),
    "ident": ("sbuf", [128, 128], "float32"),
    "send": ("sbuf", [128, W], "float32"),
    "hland": ("sbuf", [128, MAXSRC * W], "float32"),
    "land": ("sbuf", [128, (SIDE + 2) * WP], "float32"),
    "tmp": ("sbuf", [128, 128], "float32"),
    "tmp2": ("sbuf", [128, 128], "float32"),
    "cc": ("sbuf", [128, 1], "float32"),
    "rc": ("sbuf", [128, 1], "float32"),
    "dc2": ("sbuf", [128, 128], "float32"),
    "at": ("sbuf", [128, 1], "float32"),
    "ra": ("sbuf", [128, 1], "float32"),
    "rep": ("sbuf", [128, 128], "float32"),
    "diag": ("sbuf", [128, 128], "float32"),
    "yo": ("sbuf", [128, 128], "float32"),
    "psP": ("psum", [128, 512], "float32"),
    "psA": ("psum", [128, 512], "float32"),
    "psS": ("psum", [128, 512], "float32"),
}
SEMAPHORES = ["cst", "idn", "ldx", "ldw", "xarr", "sqd", "mmP", "mmA", "blk", "sent", "harr", "hsent", "arr",
              "f_c", "f_rc", "f_k", "f_pre", "f_at", "f_ra", "f_t1", "f_t2", "f_dg", "f_S", "f_y", "sty"]


def _bits(mask):
    return [b for b in range(mask.bit_length()) if (mask >> b) & 1]


def _pick(mask, n, taken=0):
    m = 0
    for b in _bits(mask & ~taken)[:n]:
        m |= 1 << b
    return m


def _plan(T, topo):
    cores = list(T.cores)
    chip_of = [topo.chip(c) for c in cores]
    planes = []
    for r, ch in enumerate(chip_of):
        for p in planes:
            if chip_of[p[0]] == ch or topo.same_plane(chip_of[p[0]], ch):
                p.append(r)
                break
        else:
            planes.append([r])
    sites = []
    for ch in chip_of:
        pr = sorted([ch] + [m for m in range(topo.CHIPS) if topo.mates(ch, m)])
        if pr not in sites:
            sites.append(pr)
    ns = len(sites)
    at_site = [[r for r in range(len(cores)) if chip_of[r] in pr] for pr in sites]
    every = range(topo.CHIPS * topo.CORES_PER_CHIP)
    send, role = {}, {}
    for p, members in enumerate(planes):
        c0 = chip_of[members[0]]
        die = topo.die(cores[members[0]])
        chips = [[ch for ch in pr if ch == c0 or topo.same_plane(ch, c0)][0] for pr in sites]

        def free(ch, dests, same=True):
            return [c for c in every if topo.chip(c) == ch and c not in cores and c not in role
                    and (topo.die(c) == die) == same and all(topo.may_write(c, cores[d]) for d in dests)][0]

        adder = []
        for i in range(ns):
            adder.append(free(chips[i], at_site[i]))
            role[adder[i]] = (p, [], list(at_site[i]))
        for r in members:
            i = chips.index(chip_of[r])
            off = [adder[(i + k) % ns] for k in range(1, NADD + 1)]
            for c in off + [adder[i]]:
                role[c][1].append(r)
            raw = [d for k in range(NADD + 1, ns) for d in at_site[(i + k) % ns]]
            across = [d for d in raw if d not in members]
            f = free(chip_of[r], across[:1])
            role[f] = (p, [r], across[:1])
            f2 = None
            if across[1:]:
                f2 = free(chip_of[r], across[1:], False)
                role[f2] = (p, [r], across[1:])
            send[r] = (off, f, [d for d in raw if d in members], adder[i], f2)
    nl = [0] * len(cores)
    for c in sorted(role):
        p, srcs, outs = role[c]
        new = []
        for d in outs:
            new.append((d, nl[d]))
            nl[d] += 1
        role[c] = (p, srcs, new)
    many = [sum(d in send[r][2] for r in send) for d in range(len(cores))]
    seen = [0] * len(cores)
    for r in sorted(send):
        off, f, straight, own, f2 = send[r]
        new = []
        for d in straight:
            new.append((d, nl[d] if many[d] == 1 else SIDE + seen[d]))
            seen[d] += 1
        send[r] = (off, f, new, own, f2)
    return cores, planes, send, role, nl


def _masks(topo, me):
    every = range(topo.CHIPS * topo.CORES_PER_CHIP)
    far = [c for c in every if topo.chip(c) != topo.chip(me)][0]
    near = [c for c in every if topo.chip(c) == topo.chip(me) and c != me][0]
    return _pick(topo.mask(me, far), ENG), _pick(topo.mask(me, near), ENG, topo.mask(me, far))


def _dst(topo, c):
    rid, pid, _ = topo.addr(c)
    return DstId(rid=rid, pnc=pid)


def _block(g, T, n, have_x, have_xw, ncst):
    S = T.sem
    V, A, PE = g.vector, g.scalar, g.tensor
    for sem, v in have_x:
        A.wait_ge(sem, v)
    A.activation(T.xsq[:, :], T.xs[:, :], ActivationFunctionType.Square).then_inc(S.sqd, 1)
    for sem, v in have_xw:
        PE.wait_ge(sem, v)
    PE.matmul(T.psP[:, 0:128], T.ws[:, :], T.xs[:, :], start=True, stop=True).then_inc(S.mmP, 1)
    PE.wait_ge(S.sqd, 1)
    PE.wait_ge(S.cst, ncst)
    PE.matmul(T.psA[:, 0:1], T.xsq[:, :], T.onec[:, :], start=True, stop=True).then_inc(S.mmA, 1)
    V.wait_ge(S.mmP, 1)
    V.tensor_copy(T.send[:, 0:128], T.psP[:, 0:128]).then_inc(S.blk, 1)
    V.wait_ge(S.mmA, 1)
    V.tensor_scalar(T.send[:, 128:129], T.psA[:, 0:1], EPS / n, None, AluOpType.add).then_inc(S.blk, 1)


def rank_program(g, core, T, topo):
    cores, planes, send, role, nl = _plan(T, topo)
    S = T.sem
    n = len(cores)
    rank = T.rank_of(core)
    m_off, m_on = _masks(topo, core)
    half = ENG // 2
    m_x = _pick(m_on, half)
    m_w = _pick(m_on, half, m_x)
    ADD, MUL = AluOpType.add, AluOpType.mult
    SQRT = ActivationFunctionType.Sqrt

    def hblk(s):
        return T.hland[:, s * W:(s + 1) * W]

    def lblk(s):
        return T.land[:, s * WP:s * WP + W]

    if rank is None:
        if core not in role:
            return
        p, srcs, outs = role[core]
        if core in [send[r][1] for r in send]:
            g.vector.memset(T.onec[:, :], 1.0 / (128 * n)).then_inc(S.cst, 1)
            _block(g, T, n, [(S.xarr, 2 * half)], [(S.xarr, 2 * half)], 1)
            g.wait_ge(S.blk, 2)
            aps = [T.send[:, :]]
        else:
            g.wait_ge(S.harr, ENG * len(srcs))
            aps = [hblk(planes[p].index(r)) for r in srcs]
        trs = []
        for m, here in ((m_off, False), (m_on, True)):
            sel = [(d, s) for d, s in outs if (topo.chip(cores[d]) == topo.chip(core)) == here]
            if sel:
                ids = [_dst(topo, cores[d]) for d, s in sel]
                out = [lblk(s) for d, s in sel]
                if len(aps) > 1:
                    trs.append(RemoteDMATransfer(dst_ids=ids, dma_engine_mask=m, remote_sem=S.arr, srcs=aps,
                                                 dsts=out, alu_op=1))
                else:
                    trs.append(RemoteDMATransfer(dst_ids=ids, dma_engine_mask=m, remote_sem=S.arr, src=aps[0],
                                                 dsts=out))
        g.remote_dma_fused(trs, local_sem=S.hsent)
        g.wait_ge(S.hsent, ENG * len(trs))
        return

    p = [i for i, mem in enumerate(planes) if rank in mem][0]
    mine = planes[p].index(rank)
    V, A, PE, SP = g.vector, g.scalar, g.tensor, g.sync
    off, twin, straight, own, fwd = send[rank]

    SP.dma_start(T.xs[:, :], T.x[:, :]).then_inc(S.ldx, 16)
    A.dma_start(T.ws[:, :], T.w[:, :]).then_inc(S.ldw, 16)
    V.memset(T.onec[:, :], 1.0 / (128 * n)).then_inc(S.cst, 1)
    V.memset(T.ones[:, :], 1.0).then_inc(S.cst, 1)
    V.wait_ge(S.cst, 2)
    g.wait_ge(S.cst, 2)
    g.affine_select(T.ident[:, :], T.ones[:, :], [[-1, 128]], AluOpType.is_equal, 0.0, 0, 1).then_inc(S.idn, 1)

    g.wait_ge(S.ldx, 16)
    g.wait_ge(S.ldw, 16)
    g.remote_dma_fused([
        RemoteDMATransfer(dst_ids=[_dst(topo, twin)], dma_engine_mask=m_x, remote_sem=S.xarr, src=T.xs[:, :],
                          dsts=[T.xs[:, :]]),
        RemoteDMATransfer(dst_ids=[_dst(topo, twin)], dma_engine_mask=m_w, remote_sem=S.xarr, src=T.ws[:, :],
                          dsts=[T.ws[:, :]]),
    ], local_sem=S.sent)

    _block(g, T, n, [(S.ldx, 16)], [(S.ldx, 16), (S.ldw, 16)], 2)

    g.wait_ge(S.blk, 2)
    near = ([fwd] if fwd is not None else []) + [own]
    g.remote_dma_fused([
        RemoteDMATransfer(dst_ids=[_dst(topo, c) for c in off] + [_dst(topo, cores[d]) for d, s in straight],
                          dma_engine_mask=m_off, remote_sem=S.harr, src=T.send[:, :],
                          dsts=[hblk(mine) for c in off] + [lblk(s) for d, s in straight]),
        RemoteDMATransfer(dst_ids=[_dst(topo, c) for c in near], dma_engine_mask=m_on, remote_sem=S.harr,
                          src=T.send[:, :], dsts=[hblk(mine) for c in near]),
    ], local_sem=S.sent)

    A.wait_ge(S.blk, 2)
    A.activation(T.cc[:, :], T.send[:, 128:129], SQRT).then_inc(S.f_c, 1)
    V.wait_ge(S.f_c, 1)
    V.wait_ge(S.idn, 1)
    V.reciprocal(T.rc[:, :], T.cc[:, :]).then_inc(S.f_rc, 1)
    V.tensor_scalar(T.dc2[:, :], T.ident[:, :], T.cc[:, 0:1], T.cc[:, 0:1], MUL, MUL).then_inc(S.f_k, 1)
    V.wait_ge(S.f_rc, 1)
    V.tensor_scalar(T.rep[:, :], T.ones[:, :], T.rc[:, 0:1], None, MUL).then_inc(S.f_k, 1)
    A.wait_ge(S.f_k, 2)
    PE.wait_ge(S.f_k, 2)

    k = nl[rank]
    early = sum(d == rank for r in send for d, s in send[r][2])
    V.wait_ge(S.harr, ENG * early)
    if early > 1:
        V.tensor_tensor(lblk(k), lblk(SIDE), lblk(SIDE + 1), ADD).then_inc(S.f_pre, 1)
        V.wait_ge(S.f_pre, 1)
    P = [T.land[:, s * WP:s * WP + 128] for s in range(k + 1)]

    V.wait_ge(S.arr, ENG * k)
    V.tensor_reduce(T.at[:, :], T.land[:, 128:k * WP + W:WP], AxisListType.X, ADD).then_inc(S.f_at, 1)
    V.tensor_tensor(T.tmp2[:, :], P[k], P[k - 1], ADD).then_inc(S.f_t2, 1)
    V.wait_ge(S.f_at, 1)
    V.reciprocal(T.ra[:, :], T.at[:, :]).then_inc(S.f_ra, 1)
    A.wait_ge(S.f_ra, 1)
    A.activation(T.diag[:, :], T.dc2[:, :], SQRT, scale=T.ra[:, 0:1]).then_inc(S.f_dg, 1)
    PE.wait_ge(S.f_dg, 1)
    PE.matmul(T.psS[:, 0:128], T.rep[:, :], T.diag[:, :], start=True, stop=True).then_inc(S.f_S, 1)
    V.tensor_tensor(T.tmp[:, :], P[0], P[1], ADD).then_inc(S.f_t1, 1)
    V.wait_ge(S.f_t2, 1)
    t2 = 1
    for s in range(2, k - 1):
        V.tensor_tensor(T.tmp2[:, :], T.tmp2[:, :], P[s], ADD).then_inc(S.f_t2, 1)
        t2 += 1
        V.wait_ge(S.f_t2, t2)
    V.wait_ge(S.f_t1, 1)
    V.tensor_tensor(T.tmp[:, :], T.tmp[:, :], T.tmp2[:, :], ADD).then_inc(S.f_t1, 1)
    V.wait_ge(S.f_t1, 2)
    V.wait_ge(S.f_S, 1)
    V.tensor_tensor(T.yo[:, :], T.tmp[:, :], T.psS[:, 0:128], MUL).then_inc(S.f_y, 1)
    SP.wait_ge(S.f_y, 1)
    SP.dma_start(T.y[:, :], T.yo[:, :]).then_inc(S.sty, 16)
    SP.wait_ge(S.sty, 16)
    g.wait_ge(S.sent, 2 * half + 2 * ENG)
